import numpy as np, ml_dtypes
CORES = [16,18,20,22]
N = 4
import mx_ref
BF = ml_dtypes.bfloat16
def gentries(a):
    return np.ascontiguousarray(a.reshape(8, 16, -1).transpose(0, 2, 1)).reshape(8, -1)
def gtable(e):
    e = np.asarray(e); return np.ascontiguousarray(e.reshape(8, -1, 16).transpose(0, 2, 1)).reshape(128, -1).astype(np.int32)
def gcols(t, e):
    v = np.concatenate([t.reshape(8, 16, -1, 4), np.zeros((8, 16, 1, 4), BF)], axis=2)
    return np.ascontiguousarray(np.stack([v[g][:, e[g]] for g in range(8)])).reshape(128, -1)
def tile(rs):
    return np.stack(rs, axis=2).reshape(128, -1).astype(BF)
def pick(q, e):
    c = np.concatenate([q[0].reshape(128, -1, 4), np.zeros((128, 1, 4), np.uint8)], axis=1); s = np.concatenate([q[1], np.ones((16, 1), np.uint8)], axis=1)
    return (np.ascontiguousarray(c[:, e].reshape(128, -1)), np.ascontiguousarray(s[:, e]))
def join(*qs):
    return (np.concatenate([q[0] for q in qs], axis=1), np.concatenate([q[1] for q in qs], axis=1))
def put(q, e, v):
    c, s = q[0].reshape(128, -1, 4).copy(), q[1].copy(); c[:, e] = v[0].reshape(128, -1, 4); s[:, e] = v[1]
    return (c.reshape(128, -1), s)
def pk(c, s):
    return (np.ascontiguousarray(c), mx_ref.live(s))
def emit(q):
    return q[0], q[1]
def packed(v, rng):
    q = [mx_ref.quantize(np.ascontiguousarray(v[r])) for r in range(N)]
    return np.stack([a for a, b in q]), np.stack([mx_ref.plane(b, rng) for a, b in q])
def values_of_codes():
    e, c = np.zeros((128, 128, 4), np.float32), np.zeros((128, 2, 4), np.uint8)
    e[np.arange(128), np.arange(128), 0] = 1
    c[:127, :, 0] = np.arange(256).reshape(2, 128).T[:127]
    return mx_ref.matmul(mx_ref.quantize(e.reshape(128, 512).astype(BF)), (c.reshape(128, 8), np.full((16, 2), 127, np.uint8))).T.reshape(-1).astype(np.float64)
CODE_VALUE, SCALE_VALUE = values_of_codes(), 2.0 ** (np.arange(256) - 127.0)
def decode(q):
    return (CODE_VALUE[q[0]].reshape(16, 8, -1, 4) * SCALE_VALUE[q[1]][:, None, :, None] + 0.0).reshape(128, -1).astype(np.float32)
def f(rng, *shape):
    return mx_ref.flush((rng.standard_normal(shape, dtype=np.float32) * np.exp2(rng.integers(-2, 3, shape[:-1] + (1,)))).astype(BF))
def wide(rng, *shape, cols=0):
    v = rng.standard_normal(shape, dtype=np.float32) * np.exp2(rng.integers(-12, 13, shape)).astype(np.float32)
    if cols: v *= np.repeat(np.exp2(rng.integers(-cols, cols + 1, shape[:-2] + (1, shape[-1] // 4))) * (rng.random(shape[:-2] + (1, shape[-1] // 4)) > 0.0625), 4, axis=-1).astype(np.float32)
    return mx_ref.flush(v.astype(BF))
C = 448
STEP = [1, 2, 3]
def numbers_of(rng):
    return {"x": np.array(f(rng, N, 128, 4 * C)), "u": np.array(f(rng, N, 128, 512)), "v": np.array(f(rng, N, 128, 512))}
def stored(h, t):
    return {"hl": np.stack([gtable(h[r]) for r in range(N)]), "tl": np.stack([gtable(t[r]) for r in range(N)])}
def lists(rng):
    e = np.tile(np.arange(C), (N, 8, 1))
    return stored(rng.permuted(e, axis=2), rng.permuted(e, axis=2))
def layers(rng, still=()):
    w = np.array(f(rng, N, 128, 2048)).reshape(N, 8, 16, 4, 8, 16, 4)
    for i in still:
        w[:, :, i] = 0
        w[:, :, :, :, :, i] = 0
    return w
def weights(rng, w):
    c, s = packed(np.ascontiguousarray(w).reshape(N, 128, 2048), rng)
    return {"wc": c, "ws": s}
def setup_inputs(rng):
    return {**numbers_of(rng), **lists(rng), **weights(rng, layers(rng))}
def setup_inputs_ties(rng):
    d = numbers_of(rng)
    o = rng.permutation(N)
    k = rng.integers(0, 4, (N, 2, 8, C))
    k[o[1]] += 1
    for g in rng.permutation(8)[:4]: k[o[2], :, g] = 1
    x = d["x"].reshape(N, 8, 16, C, 4)
    u = d["u"].reshape(N, 128, 128, 4)
    for i in range(2):
        x[:, :, i] = 0
        x[:, :, i, :, 0] = k[:, i].astype(np.float32).astype(BF)
        u[:, :, i::16] = 0
        for r in range(N):
            for h in range(i, 128, 16): u[r, h, h, 0] = 0.0 if r == o[0] else -1.0 if r == o[1] else 1.0
    a = np.exp2(rng.integers(-3, 4, (8, 1)).astype(np.float32))
    x[:, :, 8:] = 0
    x[:, :, 8, :, 0] = (-1.125 * a).astype(BF)
    x[:, :, 10, :, 0] = (-0.0703125 * a).astype(BF)
    w = layers(rng, [0, 1])
    w[:, :, :, :, :, 8:] = 0
    for g in range(8):
        w[:, g, 8, 0, g, 8, 0] = -28.0
        for b in range(4): w[:, g, 10, b, g, 9, 0] = -2.0 ** (b - 5)
    return {"x": x.reshape(N, 128, 4 * C), "u": u.reshape(N, 128, 512), "v": d["v"], **lists(rng), **weights(rng, w)}
def setup_inputs_near(rng):
    d = numbers_of(rng)
    x = d["x"].astype(np.float32).reshape(N, 8, 16, C, 4)
    x[:, :, 0] = 0
    x[:, :, 8:] = 0
    u = d["u"].reshape(N, 128, 128, 4)
    for i in range(2): u[:, :, i::16] = 0
    w = layers(rng, [0, 8, 9, 10, 11, 12, 13, 14, 15])
    o = rng.permutation(N) % 4
    for r in range(N):
        c = rng.choice([-1.0, 1.0], (8, 1))
        k = 1.0 if o[r] == 0 else 2.0 ** -30
        if o[r] < 2:
            x[r, :, 0, :, 0] = c
            x[r, :, 11, :, 0] = 2.0 ** -10
        x[r, :, 13, :, 0] = rng.integers(0, 2, (8, C)) * (2.0 ** -20 if o[r] < 2 else 2.0 ** -30)
        x[r, :, 15, :, 0] = 2.0 ** -20 if o[r] < 2 else 2.0 ** -29
        for g in range(8):
            w[r, g, 13, 0, g, 12, 0] = 2.0 ** -18 if o[r] < 2 else 2.0 ** -8
            if o[r] < 2: w[r, g, 14, 0, g, 12, 0] = 2.0 ** -6
            w[r, g, 15, 0, g, 15, 0] = 2.0 ** -5 if o[r] < 2 else 16.0
        for i in range(2):
            s = rng.integers(0, 16, (8, C))
            digits = ((s[:, :, None] >> np.arange(4)) & 1) * np.exp2(np.arange(4) - 23.0)
            if o[r] < 2: x[r, :, 8 + i] = digits
            elif o[r] == 2: x[r, :, 8 + i] = digits * rng.choice([-1.0, 1.0], (8, C, 1))
            else:
                x[r, :, 8 + 2 * i, :, 0] = np.where(s < 8, 1.25, 0.0) * 2.0 ** -30 * c
                x[r, :, 9 + 2 * i, :, 0] = np.where(s < 8, 0.0, 1.125) * 2.0 ** -30 * c
                for g in rng.permutation(8)[:4]:
                    e = rng.choice([-1.0, 1.0], C) * 2.0 ** -30
                    x[r, g, 8 + 2 * i, :, 0] = 1.25 * e
                    x[r, g, 9 + 2 * i, :, 0] = -1.125 * e
            for p in range(0, 128, 16):
                u[r, p, p + i, 0] = k if o[r] < 2 else 1.0
                u[r, p + 12, p + i, 0] = k
                if o[r] < 2: u[r, p + 11, p + i, 0] = k
                if o[r] < 3: u[r, p + 8 + i, p + i] = k
                else:
                    u[r, p + 8 + 2 * i, p + i, 0] = k
                    u[r, p + 9 + 2 * i, p + i, 0] = 1.125 * k
        at = [0, C - 1, int(rng.integers(C)), int(rng.integers(C))]
        for g, j in zip(rng.permutation(8)[:4], at): x[r, g, 0, j, 0] = 2.0 ** 29 * rng.choice([-1.0, 1.0])
    return {"x": x.reshape(N, 128, 4 * C).astype(BF), "u": u.reshape(N, 128, 512), "v": d["v"], **lists(rng), **weights(rng, w)}
def setup_inputs_odd(rng):
    d = numbers_of(rng)
    x = (1.0 + (2 * rng.integers(0, 64, (N, 16, 8, C, 4)) + 1) * 2.0 ** -7) * np.exp2(-rng.integers(0, 7, (N, 16, 8, C, 4)).astype(np.float64)) * rng.choice([-1.0, 1.0], (N, 16, 8, C, 4))
    x[:, :, 0, :, 0] = 1.96875 * 2.0 ** 8 * rng.choice([-1.0, 1.0], (N, 16, 1))
    u = d["u"].reshape(N, 128, 128, 4)
    for i in range(2):
        x[:, ::2, 1 + i, :, 0] = (8 + rng.integers(0, 2, (N, 8, C))) * 2.0 ** -8
        u[:, :, i::16] = 0
        for h in range(i, 128, 16): u[:, h + 1, h, 0] = 1.0
    return {"x": x.astype(np.float32).reshape(N, 128, 4 * C).astype(BF), "u": u.reshape(N, 128, 512), "v": d["v"], **lists(rng), **weights(rng, layers(rng, [0, 8]))}
def setup_inputs_ends(rng):
    d = numbers_of(rng)
    x = np.zeros((N, 8, 16, C, 4))
    u = d["u"].astype(np.float32).reshape(N, 128, 128, 4)
    v = d["v"].astype(np.float32)
    w = np.zeros((N, 128, 4, 128, 4), np.float32)
    hh, tt = np.zeros((N, 8, C), np.int64), np.zeros((N, 8, C), np.int64)
    o, e = rng.permutation(N) % 4, rng.permutation(N) % 4
    i, a = np.arange(128), np.arange(C)
    for r in range(N):
        low = -(0.8 + 0.08 * rng.random((8, 16, C, 4))) * 2.0 ** 30
        low[:, 15] = -2.0 ** 30
        tiny = -(1.0 + 0.125 * rng.integers(0, 8, (8, 16, C, 4))) * 2.0 ** -30
        if o[r] == 0: x[r] = low
        if o[r] == 1: x[r] = np.where((rng.random(C) < 0.5)[:, None], -low, low)
        if o[r] == 2: x[r] = tiny
        if o[r] == 3: x[r] = d["x"][r].astype(np.float32).reshape(8, 16, C, 4)[:, :, :1]
        x[r, 0] = tiny[0] * 2.0 ** 20 if o[r] < 2 else tiny[0] if o[r] == 2 else -2.0 ** -30
        for k in range(2):
            h = rng.permutation(8)
            c = np.where(h < 2, 0.0, h % 2 * 2.0 - 1.0)[None, :, None]
            if o[r] < 2: u[r, :, k::16] = c * (0.9 + 0.1 * rng.random((128, 8, 4))) * 2.0 ** 30
            if o[r] == 2: u[r, :, k::16] = c * (1.0 + 0.125 * rng.integers(0, 8, (128, 8, 4))) * 2.0 ** -30
            if o[r] == 3: u[r, :, k::16] *= np.abs(c).astype(np.float32)
        if o[r] < 2: v[r] = rng.choice([-1.0, 1.0], (128, 512)) * (0.9 + 0.1 * rng.random((128, 512))) * 2.0 ** 30
        else: v[r] = rng.choice([-1.0, 1.0], (128, 512)) * (1.0 + 0.125 * rng.integers(0, 8, (128, 512))) * 2.0 ** -30
        k = np.array([0.25, 0.5, 1.0])[rng.permutation(8) % 3] * rng.choice([-1.0, 1.0], 8)
        if o[r] == 2: k[:] = 0.0
        k[0] = 2.0 ** 8 if o[r] > 1 else 2.0 ** -8
        for b in range(4): w[r, i, b, i, b] = np.where((i >= 16) & (i % 16 == 15), 0.0, k[i // 16])
        hh[r] = C - 1 - a if e[r] == 1 else a
        if e[r] == 3: hh[r] = rng.permuted(np.tile(a, (8, 1)), axis=1)
        tt[r] = hh[r] if e[r] < 2 else np.roll(a, 1) if e[r] == 2 else hh[r] ^ 1
    return {"x": x.astype(np.float32).reshape(N, 128, 4 * C).astype(BF), "u": u.reshape(N, 128, 512).astype(BF), "v": v.astype(BF), **stored(hh, tt), **weights(rng, w.astype(BF))}
def setup_inputs_spread(rng):
    d = setup_inputs(rng)
    d["x"] = wide(rng, N, 128, 4 * C, cols=6)
    return d
def check_inputs(d):
    b = []
    for k in ("x", "u", "v"):
        a = np.abs(d[k].astype(np.float32))
        if not (np.isfinite(a).all() and ((a == 0) | (a >= 2.0 ** -30) & (a <= 2.0 ** 30)).all()): b.append("a value of " + k)
    for k in ("hl", "tl"):
        for r in range(N):
            if not (np.sort(gentries(d[k][r]), axis=1) == np.arange(C)).all(): b.append(k + ": every number once in a group")
    none, least, most = [emit(mx_ref.quantize(np.full((128, 16), k, np.float32).astype(BF)))[1][0, 0] for k in (0.0, 2.0 ** -8, 2.0 ** 8)]
    for r in range(N):
        if ((d["wc"][r] == 0x7F) | (d["wc"][r] == 0xFF)).any(): b.append("wc: a code that is no number")
        s = mx_ref.live(d["ws"][r])
        if ((s != none) & ((s < least) | (s > most))).any(): b.append("ws: a scale out of range")
    return b
def ordered(s, a):
    e = np.sort(np.argsort(a, axis=1).reshape(8, -1, 2), axis=2)
    k = np.take_along_axis(s, e.reshape(8, -1), axis=1).reshape(e.shape)
    return np.where((k[:, :, 1] > k[:, :, 0])[:, :, None], e[:, :, ::-1], e).reshape(8, -1)
def transition(s, h, t):
    m = np.zeros((8, C), np.int64)
    np.put_along_axis(m, ordered(s, h), ordered(s, t), axis=1)
    return m
def behind(a, e):
    return np.take_along_axis(a, e, axis=1)
def reference(x, u, v, hl, tl, wc, ws):
    qu = [mx_ref.quantize(u[r]) for r in range(N)]
    lay = [pk(wc[r], ws[r]) for r in range(N)]
    now = [x[r] for r in range(N)]
    head, tail = [gentries(hl[r]) for r in range(N)], [gentries(tl[r]) for r in range(N)]
    for step in STEP:
        way, made = [], []
        for r in range(N):
            s = mx_ref.matmul(qu[r], mx_ref.quantize(now[r])) + np.float32(0.0)
            m0, m1 = transition(s[0::16], head[r], tail[r]), transition(s[1::16], head[r], tail[r])
            way.append(behind(m1, m0))
            z = mx_ref.quantize(((gcols(now[r], m0).astype(np.float32) + gcols(now[r], way[r]).astype(np.float32)) * np.float32(0.5)).astype(BF))
            made.append(mx_ref.quantize(tile([mx_ref.matmul(pick(lay[r], np.arange(128 * b, 128 * b + 128)), z) * np.float32(0.03125) for b in range(4)])))
        for r in range(N):
            p = r ^ step
            far = gcols(decode(made[p]).astype(BF), behind(way[r], way[p]))
            now[r] = (now[r].astype(np.float32) + far.astype(np.float32)).astype(BF)
            head[r], tail[r] = tail[r], behind(head[r], way[p])
    y, tp = np.zeros((N, 128, C), np.float32), np.zeros((N, 8, C), np.float32)
    oc, osc = np.zeros((N, 128, 4 * C), np.uint8), np.zeros((N, 16, C), np.uint8)
    for r in range(N):
        q = mx_ref.quantize(now[r])
        y[r] = mx_ref.matmul(mx_ref.quantize(v[r]), q)
        tp[r] = tail[r]
        oc[r], osc[r] = emit(q)
    return {"y": y, "tp": tp, "oc": oc, "osc": osc}

@@ -1,0 +1,400 @@
+from concourse.mybir import dt, AluOpType, ActivationFunctionType
+
+C = 448
+STEP = [1, 2, 3]
+RUNS = [(0, 224), (224, 448)]
+LIN = 464
+TW = 928
+A_, B_, LO_, HI_, HS_, LT_ = 0, 1, 2, 3, 4, 5
+
+
+def _bf(n):
+    return ("sbuf", [128, n], "bfloat16")
+
+
+def _codes(n):
+    return ("sbuf", [128, n], "float8_e4m3fn_x4")
+
+
+def _plane(n):
+    return ("sbuf", [128, n], "uint8")
+
+
+def _sb(n, d):
+    return ("sbuf", [128, n], d)
+
+
+SCRATCH = {
+    "hin": _sb(28, "int32"), "tin": _sb(28, "int32"),
+    "ut": _bf(512), "vt": _bf(512), "ones": _bf(512), "et": _bf(2048),
+    "xs": _bf(4 * 1792), "xp": _bf(3 * 1792), "yf": _sb(3 * 1792, "float32"),
+    "zt": _bf(3 * 1792), "ht": _bf(3 * 1792), "dp": _bf(3 * 1792),
+    "qu": _codes(128), "su": _plane(128), "qv": _codes(128), "sv": _plane(128),
+    "wq": _codes(512), "wp": _plane(512), "qe": _codes(512), "se": _plane(512),
+    "qx": _codes(4 * 448), "sx": _plane(4 * 448), "qz": _codes(3 * 448), "sz": _plane(3 * 448),
+    "qh": _codes(3 * 448), "sh": _plane(3 * 448), "qa": _codes(3 * 448), "sa": _plane(3 * 448),
+    "sf": _sb(3 * 448, "float32"), "sg": _sb(3 * 448, "float32"), "slo": _sb(3 * 448, "float32"),
+    "iot": _bf(448), "ln": _bf(8 * LIN + 16), "tt": _bf(6 * TW), "tinv": _bf(4 * 448), "lg": _bf(12 * 448),
+    "seli": _sb(64, "int32"), "sel": _sb(4, "uint16"), "pg": _sb(4, "float32"),
+    "li": _sb(512, "int32"), "lu": _sb(1024, "uint16"), "lf": _sb(2560, "float32"), "bt": _bf(192),
+    "mu": _sb(192, "uint16"), "ma": _sb(192, "uint16"),
+    "tpf": _sb(448, "float32"), "yo": _sb(448, "float32"),
+    "ps": ("psum", [128, 4096], "float32"),
+}
+SEMAPHORES = (["cv", "cs", "ct", "cp", "loc", "ltl", "lhl", "lxx", "luu", "lww", "lvv", "lane", "outs"]
+              + ["ml%d" % n for n in range(3)] + ["ar%d%d" % (n, h) for n in range(3) for h in range(2)])
+
+
+def rank_program(g, core, T, topo):
+    rank = T.rank_of(core)
+    if rank is None:
+        return
+    OP, AF = AluOpType, ActivationFunctionType
+    V, S, PE, Y = g.vector, g.scalar, g.tensor, g.sync
+    Q = {"v": V, "s": S, "t": PE, "p": g, "y": Y}
+    cnt = {"v": 0, "s": 0, "t": 0, "p": 0}
+    seen = {q: {} for q in Q}
+    ncl = {"i": 0, "u": 0, "f": 0}
+    tabs = {"i": T.li, "u": T.lu, "f": T.lf}
+
+    def need(q, *toks):
+        best = {}
+        for t in toks:
+            for a in (t if isinstance(t, list) else [t]):
+                if a is not None:
+                    best[a[0]] = max(best.get(a[0], 0), a[1])
+        for k, v in best.items():
+            if seen[q].get(k, 0) < v:
+                Q[q].wait_ge(T.sem[k], v)
+                seen[q][k] = v
+
+    def done(q, inst):
+        cnt[q] += 1
+        inst.then_inc(T.sem["c" + q], 1)
+        return ("c" + q, cnt[q])
+
+    def take(k, n):
+        a = ncl[k]
+        ncl[k] = a + n
+        return a
+
+    def cols(k, n):
+        a = take(k, n)
+        return tabs[k][:, a:a + n]
+
+    def vts(out, in0, s1, op0, deps, s2=None, op1=None):
+        need("v", *deps)
+        if op1 is None:
+            return done("v", V.tensor_scalar(out, in0, s1, None, op0))
+        return done("v", V.tensor_scalar(out, in0, s1, s2, op0, op1))
+
+    def vtt(out, in0, in1, op, deps):
+        need("v", *deps)
+        return done("v", V.tensor_tensor(out, in0, in1, op))
+
+    def vcp(out, in_, deps):
+        need("v", *deps)
+        return done("v", V.tensor_copy(out, in_))
+
+    def scp(out, in_, deps, scale=None):
+        need("s", *deps)
+        if scale is None:
+            return done("s", S.activation(out, in_, AF.Copy))
+        return done("s", S.activation(out, in_, AF.Copy, scale=scale))
+
+    def quant(qb, sb, a, b, tile, deps):
+        need("v", *deps)
+        return done("v", V.quantize_mx(qb[:, a:b], sb[:, a:b], tile))
+
+    free = [[] for _ in range(8)]
+
+    def mm(k, n, l, ls, r, rs, deps):
+        need("t", free[k], *deps)
+        free[k] = []
+        return done("t", PE.matmul_mx(T.ps[:, 512 * k:512 * k + n], l, ls, r, rs, True, True))
+
+    def bank(k, n):
+        return T.ps[:, 512 * k:512 * k + n]
+
+    def lin(k):
+        return T.ln[:, LIN * k + 16:LIN * k + LIN]
+
+    Y.dma_start(T.tin[:], T.tl[:, :]).then_inc(T.sem.ltl, 16)
+    Y.dma_start(T.hin[:], T.hl[:, :]).then_inc(T.sem.lhl, 16)
+    Y.dma_start(T.xs[:, 0:1792], T.x[:, :]).then_inc(T.sem.lxx, 16)
+    S.dma_start(T.ut[:], T.u[:, :]).then_inc(T.sem.luu, 16)
+    S.dma_start(T.wq[:, 0:512].bitcast(dt.uint8), T.wc[:, :]).then_inc(T.sem.lww, 16)
+    S.dma_start(T.wp[:], T.ws[:, :]).then_inc(T.sem.lww, 16)
+    S.dma_start(T.vt[:], T.v[:, :]).then_inc(T.sem.lvv, 16)
+    TL, HL, LX, LU, LW, LV = ("ltl", 16), ("lhl", 16), ("lxx", 16), ("luu", 16), ("lww", 32), ("lvv", 16)
+
+    def si(k):
+        return T.seli[:, 4 * k:4 * k + 4]
+    iP = done("p", g.iota(si(0), [[0, 4]], 0, 1))
+    iC = done("p", g.iota(si(1), [[0, 2], [16, 2]], 0, 0))
+    iL = done("p", g.iota(si(2), [[1, 2], [0, 2]], 0, 0))
+    tIOT = done("p", g.iota(T.iot[:], [[1, 448]], -224, 0, allow_small_or_imprecise_dtypes=True))
+    iw0 = cols("f", 64)
+    iW = done("p", g.iota(iw0, [[0, 2], [16, 32]], 0, 1, allow_small_or_imprecise_dtypes=True))
+    tONE = done("v", V.memset(T.ones[:], 1.0))
+    pads = None
+    for k in range(9):
+        pads = done("v", V.memset(T.ln[:, LIN * k:LIN * k + 16], 0.0))
+    for b in range(4):
+        need("p", tONE)
+        tE = done("p", g.affine_select(T.et[:, 512 * b:512 * b + 512], T.ones[:], [[1, 512]], OP.is_equal, 0.0, -b, -4))
+    a1 = vts(si(3), si(0), 15, OP.bitwise_and, [iP])
+    a2 = vts(si(4), si(0), 16, OP.bitwise_and, [iP])
+    a3 = vts(si(5), si(0), 4, OP.arith_shift_right, [iP])
+    a4 = vtt(si(6), si(1), si(3), OP.add, [iC, a1])
+    a5 = vtt(si(7), si(0), si(5), OP.add, [iP, a3])
+    a6 = vtt(si(8), si(4), si(2), OP.add, [iL, a2])
+    a7 = vts(si(9), si(7), 1, OP.bitwise_and, [a5])
+    a8 = vtt(si(10), si(6), si(9), OP.add, [a4, a7])
+    a9 = vts(si(11), si(9), 448, OP.mult, [a7])
+    a10 = vts(si(12), si(10), 1, OP.arith_shift_right, [a8])
+    a11 = vtt(si(13), si(8), si(11), OP.add, [a6, a9])
+    a12 = vts(si(14), si(12), 32, OP.mult, [a10])
+    a13 = vtt(T.pg[:], si(0), si(3), OP.subtract, [a1])
+    a14 = vtt(si(15), si(14), si(13), OP.add, [a12, a11])
+    IW = cols("f", 64)
+    tIW = vts(IW, iw0, T.pg[:, 0:1], OP.subtract, [iW, a13])
+    tSEL = vts(T.sel[:], si(15), TW - 1, OP.min, [a14])
+    SEL = T.sel[:, 0:4]
+
+    lastT = {}
+    lastSel = {}
+
+    def turn(k, slot, deps):
+        a, o = LIN * k, TW * slot
+        need("v", pads, lastSel.get(slot), *deps)
+        done("v", V.transpose(T.tt[:, o:o + 448], T.ln[:, a + 16:a + 464]))
+        t2 = done("v", V.transpose(T.tt[:, o + 448:o + TW], T.ln[:, a:a + 480]))
+        lastT[k] = t2
+        return t2
+
+    def picked(slot):
+        return T.tt[:, TW * slot:TW * slot + TW].indirect(SEL)
+
+    def wrap(out, slot, deps):
+        t = vts(out, picked(slot), 224.0, OP.add, [tSEL] + deps)
+        lastSel[slot] = t
+        return t
+
+    def digits(l32, deps):
+        o = {"e": cols("u", 28), "o": cols("u", 28), "x": cols("u", 28)}
+        b, e, x = cols("i", 28), cols("i", 28), cols("i", 28)
+        t1 = vts(b, l32, 1, OP.bitwise_and, deps)
+        t2 = vtt(e, l32, b, OP.subtract, [t1])
+        o["te"] = vcp(o["e"], e, [t2])
+        t3 = vtt(x, e, b, OP.subtract, [t2])
+        o["to"] = vts(o["o"], e, 1.0, OP.add, [t2])
+        o["tx"] = vts(o["x"], x, 1.0, OP.add, [t3])
+        return o
+
+    tab = [{}, {}, {}]
+
+    def sibling(n, deps):
+        d = tab[n]
+        t = turn(HS_, HS_, deps)
+        a = take("f", 64)
+        f = T.lf[:, a:a + 64]
+        t = wrap(f, HS_, [t])
+        d["hs"] = cols("u", 28)
+        d["ths"] = vcp(d["hs"], T.lf[:, a:a + 28], [t])
+        q, d["th"] = cols("f", 64), cols("f", 64)
+        t = vtt(q, f, IW, OP.is_gt, [t, tIW])
+        d["tth"] = vts(d["th"], q, 2.0 ** -92, OP.mult, [t], -2.0 ** -93, OP.add)
+
+    def outs(n, gl, gh):
+        d = tab[n]
+        t1 = turn(LO_, LO_, [gl])
+        t2 = turn(HI_, HI_, [gh])
+        p, q = cols("f", 64), cols("f", 64)
+        t1 = wrap(p, LO_, [t1])
+        t2 = wrap(q, HI_, [t2])
+        a = take("f", 128)
+        d["LO"], d["HI"] = T.lf[:, a:a + 64], T.lf[:, a + 64:a + 128]
+        d["tLO"] = vtt(d["LO"], p, q, OP.min, [t1, t2])
+        d["tHI"] = vtt(d["HI"], p, q, OP.max, [t1, t2])
+        d["lo"], d["hi"] = cols("u", 28), cols("u", 28)
+        d["tlo"] = vcp(d["lo"], T.lf[:, a:a + 28], [d["tLO"]])
+        d["thi"] = vcp(d["hi"], T.lf[:, a + 64:a + 92], [d["tHI"]])
+
+    def tinv(k):
+        return T.tinv[:, 448 * k:448 * k + 448]
+
+    tu, hu = cols("u", 28), cols("u", 28)
+    ttu = vcp(tu, T.tin[:], [TL])
+    he = digits(T.hin[:], [HL])
+    tTI = [vcp(tinv(0).indirect(tu), T.iot[:], [ttu, tIOT])]
+    thu = vcp(hu, T.hin[:], [HL])
+    tHI = vcp(tinv(3).indirect(hu), T.iot[:], [thu, tIOT])
+    gl = scp(lin(LO_), tinv(0).indirect(he["e"]), [tTI[0], he["te"], pads])
+    gh = scp(lin(HI_), tinv(0).indirect(he["o"]), [tTI[0], he["to"]])
+    gs = scp(lin(HS_), tinv(3).indirect(he["x"]), [tHI, he["tx"]])
+    tQU = quant(T.qu, T.su, 0, 128, T.ut[:], [LU])
+    tX = [[LX], [], [], []]
+    tQX = [[None, None] for _ in range(4)]
+    t0 = quant(T.qx, T.sx, 0, 448, T.xs[:, 0:1792], [LX])
+    tQX[0] = [t0, t0]
+    sft, sgt = [], []
+
+    def score(n, h):
+        c0, c1 = RUNS[h]
+        a = 448 * n
+        t = mm(4 * h, c1 - c0, T.qu[:, 0:128], T.su[:, 0:128], T.qx[:, a + c0:a + c1], T.sx[:, a + c0:a + c1],
+               [tQU, tQX[n][h]])
+        r1 = scp(T.sf[:, a + c0:a + c1], bank(4 * h, c1 - c0), [t])
+        r2 = scp(T.sg[:, a + c0:a + c1], bank(4 * h, c1 - c0), [t])
+        free[4 * h] += [r1, r2]
+        sft.append(r1)
+        sgt.append(r2)
+
+    score(0, 0)
+    score(0, 1)
+    outs(0, gl, gh)
+    sibling(0, [gs])
+
+    hlin = [T.lg[:, 448 * 9:448 * 10], T.lg[:, 448 * 10:448 * 11]]
+    hrow = [T.lg[1::16, 448 * 9:448 * 10], T.lg[1::16, 448 * 10:448 * 11], T.ln[1::16, LIN * LT_ + 16:LIN * LT_ + LIN]]
+    thl = [None, None, None]
+    nloc = [0]
+    told = {}
+
+    def send(dst, out, in_, sem):
+        rid, pid, _ = topo.addr(dst)
+        g.remote_dma(out, in_, T.sem[sem], T.sem.loc, pid, rid, topo.mask(core, dst))
+        nloc[0] += len(topo.engines(core, dst))
+
+    for n in range(3):
+        d = tab[n]
+        mate = T.cores[rank ^ STEP[n]]
+        eng = len(topo.engines(core, mate))
+        x0, a0 = 1792 * n, 448 * n
+        sf, sg, slo = T.sf[:, a0:a0 + 448], T.sg[:, a0:a0 + 448], T.slo[:, a0:a0 + 448]
+        ts = scp(slo, sf.indirect(d["lo"]), [sft, d["tlo"]])
+        tXP = []
+        for b in range(4):
+            tXP.append(scp(T.xp[:, x0 + 448 * b:x0 + 448 * b + 448], T.xs[:, x0 + b:x0 + 1792:4], [tX[n]]))
+        if n == 0:
+            thl[0] = scp(hlin[0], T.iot[:].indirect(hu), [thu, tIOT])
+        ta = vtt(lin(A_), sf.indirect(d["hs"]), sg, OP.subtract, [sft, sgt, d["ths"], lastT.get(A_), pads])
+        tb = vtt(lin(B_), sf.indirect(d["hi"]), slo, OP.is_gt, [ts, d["thi"], lastT.get(B_)])
+        ta = turn(A_, A_, [ta])
+        tb = turn(B_, B_, [tb])
+        ba = T.bt[:, 64 * n:64 * n + 64]
+        t = vtt(ba, picked(A_), d["th"], OP.is_gt, [ta, d["tth"], tSEL])
+        lastSel[A_] = t
+        e, w, m = cols("f", 64), cols("f", 64), cols("f", 64)
+        t = vtt(e, picked(B_), ba, OP.not_equal, [tb, t])
+        lastSel[B_] = t
+        t = vtt(w, e, d["HI"], OP.mult, [t, d["tHI"]])
+        t = vtt(m, w, d["LO"], OP.max, [t, d["tLO"]])
+        tm = vcp(T.mu[:, 64 * n:64 * n + 64], m, [t])
+        m0, m1 = T.mu[:, 64 * n:64 * n + 28], T.mu[:, 64 * n + 32:64 * n + 60]
+        need("p", tm)
+        send(mate, T.ma[:, 64 * n:64 * n + 64], T.mu[:, 64 * n:64 * n + 64], "ml%d" % n)
+        G = [T.lg[:, 448 * (3 * n + k):448 * (3 * n + k) + 448] for k in range(3)]
+        tg1 = scp(G[0], T.iot[:].indirect(m1), [tm, tIOT])
+        tz = []
+        for b in range(4):
+            p = x0 + 448 * b
+            yp = T.yf[:, p:p + 448]
+            ty = vtt(yp, T.xp[:, p:p + 448].indirect(m1), T.xs[:, x0 + b:x0 + 1792:4], OP.add, [tm, tXP[b], tX[n]])
+            if b < 3:
+                tz.append(scp(T.zt[:, x0 + b:x0 + 1792:4], yp.indirect(m0), [ty], scale=0.5))
+            else:
+                tza = vts(T.zt[:, x0 + b:x0 + 896:4], yp.indirect(T.mu[:, 64 * n:64 * n + 14]), 0.5, OP.mult, [ty])
+                tzb = scp(T.zt[:, x0 + 896 + b:x0 + 1792:4], yp.indirect(T.mu[:, 64 * n + 14:64 * n + 28]), [ty], scale=0.5)
+        tq = [quant(T.qz, T.sz, a0, a0 + 224, T.zt[:, x0:x0 + 896], tz + [tza]),
+              quant(T.qz, T.sz, a0 + 224, a0 + 448, T.zt[:, x0 + 896:x0 + 1792], tz + [tzb])]
+        tg2 = scp(G[1], G[0].indirect(m0), [tg1])
+        need("y", tg2, thl[n])
+        Y.dma_start(T.lg[1::16, 448 * (3 * n + 1):448 * (3 * n + 2)], hrow[n]).then_inc(T.sem.lane, 16)
+        for h in range(2):
+            c0, c1 = RUNS[h]
+            tr = [mm(b + 4 * h, c1 - c0, T.wq[:, 128 * b:128 * b + 128], T.wp[:, 128 * b:128 * b + 128],
+                     T.qz[:, a0 + c0:a0 + c1], T.sz[:, a0 + c0:a0 + c1], [LW, tq[h]]) for b in range(4)]
+            th = []
+            for b in range(4):
+                o = T.ht[:, x0 + 4 * c0 + b:x0 + 4 * c1:4]
+                if b % 2 == 0:
+                    r = vts(o, bank(b + 4 * h, c1 - c0), 0.03125, OP.mult, [tr[b]])
+                else:
+                    r = scp(o, bank(b + 4 * h, c1 - c0), [tr[b]], scale=0.03125)
+                free[b + 4 * h].append(r)
+                th.append(r)
+            r = quant(T.qh, T.sh, a0 + c0, a0 + c1, T.ht[:, x0 + 4 * c0:x0 + 4 * c1], th)
+            need("p", r)
+            send(mate, T.qa[:, a0 + c0:a0 + c1].bitcast(dt.uint8), T.qh[:, a0 + c0:a0 + c1].bitcast(dt.uint8),
+                 "ar%d%d" % (n, h))
+            send(mate, T.sa[:, a0 + c0:a0 + c1], T.sh[:, a0 + c0:a0 + c1], "ar%d%d" % (n, h))
+        if n == 0:
+            tQE = quant(T.qe, T.se, 0, 512, T.et[:], [tE])
+            tQV = quant(T.qv, T.sv, 0, 128, T.vt[:], [LV])
+            te = digits(T.tin[:], [TL])
+            thl[1] = scp(hlin[1], T.iot[:].indirect(tu), [ttu])
+        elif n == 1:
+            l32 = cols("i", 28)
+            te = digits(l32, [vcp(l32, told["u"], [told["t"]])])
+        if n < 2:
+            gs = scp(lin(HS_), tinv(n).indirect(te["x"]), [tTI[n], te["tx"], lastT[HS_]])
+            sibling(n + 1, [gs])
+        need("s", ("ml%d" % n, eng), ("lane", 16 * (n + 1)))
+        am0, am1 = T.ma[:, 64 * n:64 * n + 28], T.ma[:, 64 * n + 32:64 * n + 60]
+        t = scp(G[2], G[1].indirect(am1), [tg2])
+        tlt = scp(lin(LT_ + n), G[2].indirect(am0), [t, pads])
+        t = turn(LT_ + n, LT_, [tlt])
+        u0 = take("u", 64)
+        tl = wrap(T.lu[:, u0:u0 + 64], LT_, [t])
+        tn = T.lu[:, u0 + 32:u0 + 60]
+        told = {"u": tn, "t": tl}
+        if n == 0:
+            thl[2] = tlt
+        if n < 2:
+            tTI.append(vcp(tinv(n + 1).indirect(tn), T.iot[:], [tl]))
+        tdp = []
+        for h in range(2):
+            c0, c1 = RUNS[h]
+            need("t", ("ar%d%d" % (n, h), 2 * eng))
+            td = [mm(b + 4 * h, c1 - c0, T.qe[:, 128 * b:128 * b + 128], T.se[:, 128 * b:128 * b + 128],
+                     T.qa[:, a0 + c0:a0 + c1], T.sa[:, a0 + c0:a0 + c1], [tQE]) for b in range(4)]
+            for b in range(4):
+                r = scp(T.dp[:, x0 + 448 * b + c0:x0 + 448 * b + c1], bank(b + 4 * h, c1 - c0), [td[b]])
+                free[b + 4 * h].append(r)
+                tdp.append(r)
+        if n < 2:
+            gl = scp(lin(LO_), tinv(n + 1).indirect(te["e"]), [tTI[n + 1], te["te"], lastT[LO_]])
+            gh = scp(lin(HI_), tinv(n + 1).indirect(te["o"]), [tTI[n + 1], te["to"], lastT[HI_]])
+        else:
+            need("s", tlt)
+            ttp = done("s", S.activation(T.tpf[:], lin(LT_ + 2), AF.Identity, bias=224.0))
+            need("y", ttp)
+            Y.dma_start(T.tp[:, :], T.tpf[1::16, 0:448]).then_inc(T.sem.outs, 16)
+        x1, a1 = x0 + 1792, a0 + 448
+        sft, sgt = [], []
+        for h in range(2):
+            c0, c1 = RUNS[h]
+            ls = T.lu[:, u0 + c0 // 16:u0 + c1 // 16]
+            ta = []
+            for b in range(4):
+                ta.append(vtt(T.xs[:, x1 + 4 * c0 + b:x1 + 4 * c1:4],
+                              T.dp[:, x0 + 448 * b:x0 + 448 * b + 448].indirect(ls),
+                              T.xs[:, x0 + 4 * c0 + b:x0 + 4 * c1:4], OP.add, [tl, tdp[b], tdp[4 + b], tX[n]]))
+            tX[n + 1] += ta
+            tQX[n + 1][h] = quant(T.qx, T.sx, a1 + c0, a1 + c1, T.xs[:, x1 + 4 * c0:x1 + 4 * c1], ta)
+            if n < 2:
+                score(n + 1, h)
+            else:
+                need("y", tQX[3][h])
+                Y.dma_start(T.oc[:, 4 * c0:4 * c1], T.qx[:, a1 + c0:a1 + c1].bitcast(dt.uint8)).then_inc(T.sem.outs, 16)
+                k = mm(4 * h, c1 - c0, T.qv[:, 0:128], T.sv[:, 0:128], T.qx[:, a1 + c0:a1 + c1], T.sx[:, a1 + c0:a1 + c1],
+                       [tQV, tQX[3][h]])
+                need("s", scp(T.yo[:, c0:c1], bank(4 * h, c1 - c0), [k]))
+                S.dma_start(T.y[:, c0:c1], T.yo[:, c0:c1]).then_inc(T.sem.outs, 16)
+        if n < 2:
+            outs(n + 1, gl, gh)
+    for k in range(4):
+        Y.dma_start(T.osc[4 * k:4 * k + 4, 0:448], T.sx[32 * k:32 * k + 4, 1344:1792]).then_inc(T.sem.outs, 16)
+    need("y", ("outs", 16 * 9), ("loc", nloc[0]), ("lww", 32), ("lvv", 16), [("c" + q, cnt[q]) for q in cnt])

@@ -2,26 +2,28 @@ from concourse.mybir import dt, AluOpType, ActivationFunctionType
 
 C = 448
 STEP = [1, 2, 3]
-RUNS = [(0, 224), (224, 448)]
+R0 = 224
+RUNS = [(0, R0), (R0, C)]
+TINY, UP = 2.0 ** -91, 1024.0
 LIN = 464
 TW = 928
 A_, B_, LO_, HI_, HS_, LT_ = 0, 1, 2, 3, 4, 5
 
 
+def _sb(n, d):
+    return ("sbuf", [128, n], d)
+
+
 def _bf(n):
-    return ("sbuf", [128, n], "bfloat16")
+    return _sb(n, "bfloat16")
 
 
 def _codes(n):
-    return ("sbuf", [128, n], "float8_e4m3fn_x4")
+    return _sb(n, "float8_e4m3fn_x4")
 
 
 def _plane(n):
-    return ("sbuf", [128, n], "uint8")
-
-
-def _sb(n, d):
-    return ("sbuf", [128, n], d)
+    return _sb(n, "uint8")
 
 
 SCRATCH = {
@@ -34,15 +36,16 @@ SCRATCH = {
     "qx": _codes(4 * 448), "sx": _plane(4 * 448), "qz": _codes(3 * 448), "sz": _plane(3 * 448),
     "qh": _codes(3 * 448), "sh": _plane(3 * 448), "qa": _codes(3 * 448), "sa": _plane(3 * 448),
     "sf": _sb(3 * 448, "float32"), "sg": _sb(3 * 448, "float32"), "slo": _sb(3 * 448, "float32"),
-    "iot": _bf(448), "ln": _bf(8 * LIN + 16), "tt": _bf(6 * TW), "tinv": _bf(4 * 448), "lg": _bf(12 * 448),
-    "seli": _sb(64, "int32"), "sel": _sb(4, "uint16"), "pg": _sb(4, "float32"),
+    "iot": _bf(448), "ln": _bf(8 * LIN + 16), "tt": _bf(6 * TW), "lg": _bf(11 * 448),
+    "tinv": _bf(4 * 448), "tp2": _bf(2 * 448), "tsw": _bf(4 * 448),
+    "seli": _sb(128, "int32"), "sel": _sb(8, "uint16"), "pg": _sb(8, "float32"),
     "li": _sb(512, "int32"), "lu": _sb(1024, "uint16"), "lf": _sb(2560, "float32"), "bt": _bf(192),
     "mu": _sb(192, "uint16"), "ma": _sb(192, "uint16"),
     "tpf": _sb(448, "float32"), "yo": _sb(448, "float32"),
     "ps": ("psum", [128, 4096], "float32"),
 }
 SEMAPHORES = (["cv", "cs", "ct", "cp", "loc", "ltl", "lhl", "lxx", "luu", "lww", "lvv", "lane", "outs"]
-              + ["ml%d" % n for n in range(3)] + ["ar%d%d" % (n, h) for n in range(3) for h in range(2)])
+              + ["ml%d" % n for n in range(3)] + ["ar%d" % n for n in range(3)])
 
 
 def rank_program(g, core, T, topo):
@@ -120,8 +123,8 @@ def rank_program(g, core, T, topo):
         return T.ln[:, LIN * k + 16:LIN * k + LIN]
 
     Y.dma_start(T.tin[:], T.tl[:, :]).then_inc(T.sem.ltl, 16)
-    Y.dma_start(T.hin[:], T.hl[:, :]).then_inc(T.sem.lhl, 16)
     Y.dma_start(T.xs[:, 0:1792], T.x[:, :]).then_inc(T.sem.lxx, 16)
+    S.dma_start(T.hin[:], T.hl[:, :]).then_inc(T.sem.lhl, 16)
     S.dma_start(T.ut[:], T.u[:, :]).then_inc(T.sem.luu, 16)
     S.dma_start(T.wq[:, 0:512].bitcast(dt.uint8), T.wc[:, :]).then_inc(T.sem.lww, 16)
     S.dma_start(T.wp[:], T.ws[:, :]).then_inc(T.sem.lww, 16)
@@ -129,13 +132,13 @@ def rank_program(g, core, T, topo):
     TL, HL, LX, LU, LW, LV = ("ltl", 16), ("lhl", 16), ("lxx", 16), ("luu", 16), ("lww", 32), ("lvv", 16)
 
     def si(k):
-        return T.seli[:, 4 * k:4 * k + 4]
-    iP = done("p", g.iota(si(0), [[0, 4]], 0, 1))
-    iC = done("p", g.iota(si(1), [[0, 2], [16, 2]], 0, 0))
-    iL = done("p", g.iota(si(2), [[1, 2], [0, 2]], 0, 0))
+        return T.seli[:, 8 * k:8 * k + 8]
+    iP = done("p", g.iota(si(0), [[0, 8]], 0, 1))
+    iC = done("p", g.iota(si(1), [[0, 4], [16, 2]], 0, 0))
+    iL = done("p", g.iota(si(2), [[1, 2], [0, 4]], 0, 0))
     tIOT = done("p", g.iota(T.iot[:], [[1, 448]], -224, 0, allow_small_or_imprecise_dtypes=True))
     iw0 = cols("f", 64)
-    iW = done("p", g.iota(iw0, [[0, 2], [16, 32]], 0, 1, allow_small_or_imprecise_dtypes=True))
+    iW = done("p", g.iota(iw0, [[0, 2], [16, 32]], -224, 1, allow_small_or_imprecise_dtypes=True))
     tONE = done("v", V.memset(T.ones[:], 1.0))
     pads = None
     for k in range(9):
@@ -158,9 +161,9 @@ def rank_program(g, core, T, topo):
     a13 = vtt(T.pg[:], si(0), si(3), OP.subtract, [a1])
     a14 = vtt(si(15), si(14), si(13), OP.add, [a12, a11])
     IW = cols("f", 64)
-    tIW = vts(IW, iw0, T.pg[:, 0:1], OP.subtract, [iW, a13])
+    tIW = vts(IW, iw0, T.pg[:, 0:1], OP.subtract, [iW, a13], TINY, OP.mult)
     tSEL = vts(T.sel[:], si(15), TW - 1, OP.min, [a14])
-    SEL = T.sel[:, 0:4]
+    SEL, SEL2 = T.sel[:, 2:6], T.sel[:, 0:8]
 
     lastT = {}
     lastSel = {}
@@ -173,66 +176,72 @@ def rank_program(g, core, T, topo):
         lastT[k] = t2
         return t2
 
-    def picked(slot):
-        return T.tt[:, TW * slot:TW * slot + TW].indirect(SEL)
+    def picked(slot, table=SEL):
+        return T.tt[:, TW * slot:TW * slot + TW].indirect(table)
 
-    def wrap(out, slot, deps):
-        t = vts(out, picked(slot), 224.0, OP.add, [tSEL] + deps)
+    def wrap(out, slot, deps, table=SEL):
+        t = vts(out, picked(slot, table), 224.0, OP.add, [tSEL] + deps)
         lastSel[slot] = t
         return t
 
-    def digits(l32, deps):
-        o = {"e": cols("u", 28), "o": cols("u", 28), "x": cols("u", 28)}
-        b, e, x = cols("i", 28), cols("i", 28), cols("i", 28)
+    def firsts(l32, deps):
+        b, e, u = cols("i", 28), cols("i", 28), cols("u", 28)
         t1 = vts(b, l32, 1, OP.bitwise_and, deps)
         t2 = vtt(e, l32, b, OP.subtract, [t1])
-        o["te"] = vcp(o["e"], e, [t2])
-        t3 = vtt(x, e, b, OP.subtract, [t2])
-        o["to"] = vts(o["o"], e, 1.0, OP.add, [t2])
-        o["tx"] = vts(o["x"], x, 1.0, OP.add, [t3])
-        return o
+        return u, vcp(u, e, [t2])
 
     tab = [{}, {}, {}]
 
     def sibling(n, deps):
         d = tab[n]
         t = turn(HS_, HS_, deps)
-        a = take("f", 64)
-        f = T.lf[:, a:a + 64]
-        t = wrap(f, HS_, [t])
-        d["hs"] = cols("u", 28)
-        d["ths"] = vcp(d["hs"], T.lf[:, a:a + 28], [t])
-        q, d["th"] = cols("f", 64), cols("f", 64)
-        t = vtt(q, f, IW, OP.is_gt, [t, tIW])
-        d["tth"] = vts(d["th"], q, 2.0 ** -92, OP.mult, [t], -2.0 ** -93, OP.add)
+        a = take("u", 64)
+        d["hs"], d["th"] = T.lu[:, a:a + 28], cols("f", 64)
+        d["ths"] = vts(T.lu[:, a:a + 64], picked(HS_), 1.0 / TINY, OP.mult, [tSEL, t], 224.0, OP.add)
+        d["tth"] = vtt(d["th"], picked(HS_), IW, OP.subtract, [t, tIW])
+        lastSel[HS_] = d["tth"]
 
     def outs(n, gl, gh):
         d = tab[n]
+        a = take("f", 256)
+        p, q = T.lf[:, a:a + 64], T.lf[:, a + 64:a + 128]
         t1 = turn(LO_, LO_, [gl])
-        t2 = turn(HI_, HI_, [gh])
-        p, q = cols("f", 64), cols("f", 64)
-        t1 = wrap(p, LO_, [t1])
-        t2 = wrap(q, HI_, [t2])
-        a = take("f", 128)
-        d["LO"], d["HI"] = T.lf[:, a:a + 64], T.lf[:, a + 64:a + 128]
+        if gh is None:
+            t1 = t2 = wrap(T.lf[:, a:a + 128], LO_, [t1], SEL2)
+        else:
+            t2 = turn(HI_, HI_, [gh])
+            t1 = wrap(p, LO_, [t1])
+            t2 = wrap(q, HI_, [t2])
+        d["LO"], d["HI"] = T.lf[:, a + 128:a + 192], T.lf[:, a + 192:a + 256]
         d["tLO"] = vtt(d["LO"], p, q, OP.min, [t1, t2])
         d["tHI"] = vtt(d["HI"], p, q, OP.max, [t1, t2])
         d["lo"], d["hi"] = cols("u", 28), cols("u", 28)
-        d["tlo"] = vcp(d["lo"], T.lf[:, a:a + 28], [d["tLO"]])
-        d["thi"] = vcp(d["hi"], T.lf[:, a + 64:a + 92], [d["tHI"]])
+        d["tlo"] = vcp(d["lo"], T.lf[:, a + 128:a + 156], [d["tLO"]])
+        d["thi"] = vcp(d["hi"], T.lf[:, a + 192:a + 220], [d["tHI"]])
 
     def tinv(k):
         return T.tinv[:, 448 * k:448 * k + 448]
 
+    def siblings(k, u, deps):
+        o = 448 * k
+        t1 = scp(T.tsw[:, o:o + 448:2], T.tinv[:, o + 1:o + 448:2], deps)
+        t2 = scp(T.tsw[:, o + 1:o + 448:2], T.tinv[:, o:o + 448:2], deps)
+        return scp(lin(HS_), T.tsw[:, o:o + 448].indirect(u), [t1, t2, pads, lastT.get(HS_)], scale=TINY)
+
+    hlin = [T.lg[:, 448 * 9:448 * 10], T.lg[:, 448 * 10:448 * 11]]
+    hrow = [T.lg[1::16, 448 * 9:448 * 10], T.lg[1::16, 448 * 10:448 * 11], T.ln[1::16, LIN * LT_ + 16:LIN * LT_ + LIN]]
     tu, hu = cols("u", 28), cols("u", 28)
     ttu = vcp(tu, T.tin[:], [TL])
-    he = digits(T.hin[:], [HL])
-    tTI = [vcp(tinv(0).indirect(tu), T.iot[:], [ttu, tIOT])]
     thu = vcp(hu, T.hin[:], [HL])
+    thl = [scp(hlin[0], T.iot[:].indirect(hu), [thu, tIOT]), scp(hlin[1], T.iot[:].indirect(tu), [ttu]), None]
+    he, the = firsts(T.hin[:], [HL])
+    ho = cols("u", 28)
+    tho = vts(ho, he, 1.0, OP.add, [the])
+    tTI = [vcp(tinv(0).indirect(tu), T.iot[:], [ttu, tIOT])]
     tHI = vcp(tinv(3).indirect(hu), T.iot[:], [thu, tIOT])
-    gl = scp(lin(LO_), tinv(0).indirect(he["e"]), [tTI[0], he["te"], pads])
-    gh = scp(lin(HI_), tinv(0).indirect(he["o"]), [tTI[0], he["to"]])
-    gs = scp(lin(HS_), tinv(3).indirect(he["x"]), [tHI, he["tx"]])
+    gl = scp(lin(LO_), tinv(0).indirect(he), [tTI[0], the, pads])
+    gh = scp(lin(HI_), tinv(0).indirect(ho), [tTI[0], tho])
+    gs = siblings(3, hu, [tHI, thu])
     tQU = quant(T.qu, T.su, 0, 128, T.ut[:], [LU])
     tX = [[LX], [], [], []]
     tQX = [[None, None] for _ in range(4)]
@@ -245,8 +254,8 @@ def rank_program(g, core, T, topo):
         a = 448 * n
         t = mm(4 * h, c1 - c0, T.qu[:, 0:128], T.su[:, 0:128], T.qx[:, a + c0:a + c1], T.sx[:, a + c0:a + c1],
                [tQU, tQX[n][h]])
-        r1 = scp(T.sf[:, a + c0:a + c1], bank(4 * h, c1 - c0), [t])
-        r2 = scp(T.sg[:, a + c0:a + c1], bank(4 * h, c1 - c0), [t])
+        r1 = scp(T.sf[:, a + c0:a + c1], bank(4 * h, c1 - c0), [t], scale=UP)
+        r2 = scp(T.sg[:, a + c0:a + c1], bank(4 * h, c1 - c0), [t], scale=UP)
         free[4 * h] += [r1, r2]
         sft.append(r1)
         sgt.append(r2)
@@ -256,9 +265,6 @@ def rank_program(g, core, T, topo):
     outs(0, gl, gh)
     sibling(0, [gs])
 
-    hlin = [T.lg[:, 448 * 9:448 * 10], T.lg[:, 448 * 10:448 * 11]]
-    hrow = [T.lg[1::16, 448 * 9:448 * 10], T.lg[1::16, 448 * 10:448 * 11], T.ln[1::16, LIN * LT_ + 16:LIN * LT_ + LIN]]
-    thl = [None, None, None]
     nloc = [0]
     told = {}
 
@@ -278,7 +284,7 @@ def rank_program(g, core, T, topo):
         for b in range(4):
             tXP.append(scp(T.xp[:, x0 + 448 * b:x0 + 448 * b + 448], T.xs[:, x0 + b:x0 + 1792:4], [tX[n]]))
         if n == 0:
-            thl[0] = scp(hlin[0], T.iot[:].indirect(hu), [thu, tIOT])
+            gs = siblings(0, tu, [ttu, tTI[0]])
         ta = vtt(lin(A_), sf.indirect(d["hs"]), sg, OP.subtract, [sft, sgt, d["ths"], lastT.get(A_), pads])
         tb = vtt(lin(B_), sf.indirect(d["hi"]), slo, OP.is_gt, [ts, d["thi"], lastT.get(B_)])
         ta = turn(A_, A_, [ta])
@@ -305,10 +311,11 @@ def rank_program(g, core, T, topo):
             if b < 3:
                 tz.append(scp(T.zt[:, x0 + b:x0 + 1792:4], yp.indirect(m0), [ty], scale=0.5))
             else:
-                tza = vts(T.zt[:, x0 + b:x0 + 896:4], yp.indirect(T.mu[:, 64 * n:64 * n + 14]), 0.5, OP.mult, [ty])
-                tzb = scp(T.zt[:, x0 + 896 + b:x0 + 1792:4], yp.indirect(T.mu[:, 64 * n + 14:64 * n + 28]), [ty], scale=0.5)
-        tq = [quant(T.qz, T.sz, a0, a0 + 224, T.zt[:, x0:x0 + 896], tz + [tza]),
-              quant(T.qz, T.sz, a0 + 224, a0 + 448, T.zt[:, x0 + 896:x0 + 1792], tz + [tzb])]
+                u = 64 * n + R0 // 16
+                tza = vts(T.zt[:, x0 + b:x0 + 4 * R0:4], yp.indirect(T.mu[:, 64 * n:u]), 0.5, OP.mult, [ty])
+                tzb = scp(T.zt[:, x0 + 4 * R0 + b:x0 + 1792:4], yp.indirect(T.mu[:, u:64 * n + 28]), [ty], scale=0.5)
+        tq = [quant(T.qz, T.sz, a0, a0 + R0, T.zt[:, x0:x0 + 4 * R0], tz + [tza]),
+              quant(T.qz, T.sz, a0 + R0, a0 + 448, T.zt[:, x0 + 4 * R0:x0 + 1792], tz + [tzb])]
         tg2 = scp(G[1], G[0].indirect(m0), [tg1])
         need("y", tg2, thl[n])
         Y.dma_start(T.lg[1::16, 448 * (3 * n + 1):448 * (3 * n + 2)], hrow[n]).then_inc(T.sem.lane, 16)
@@ -319,7 +326,7 @@ def rank_program(g, core, T, topo):
             th = []
             for b in range(4):
                 o = T.ht[:, x0 + 4 * c0 + b:x0 + 4 * c1:4]
-                if b % 2 == 0:
+                if h == 0 and b < 2:
                     r = vts(o, bank(b + 4 * h, c1 - c0), 0.03125, OP.mult, [tr[b]])
                 else:
                     r = scp(o, bank(b + 4 * h, c1 - c0), [tr[b]], scale=0.03125)
@@ -327,21 +334,21 @@ def rank_program(g, core, T, topo):
                 th.append(r)
             r = quant(T.qh, T.sh, a0 + c0, a0 + c1, T.ht[:, x0 + 4 * c0:x0 + 4 * c1], th)
             need("p", r)
-            send(mate, T.qa[:, a0 + c0:a0 + c1].bitcast(dt.uint8), T.qh[:, a0 + c0:a0 + c1].bitcast(dt.uint8),
-                 "ar%d%d" % (n, h))
-            send(mate, T.sa[:, a0 + c0:a0 + c1], T.sh[:, a0 + c0:a0 + c1], "ar%d%d" % (n, h))
+            send(mate, T.qa[:, a0 + c0:a0 + c1].bitcast(dt.uint8), T.qh[:, a0 + c0:a0 + c1].bitcast(dt.uint8), "ar%d" % n)
+            if h == 0 and n == 0:
+                te = firsts(T.tin[:], [TL])
+            elif h == 0 and n == 1:
+                l32 = cols("i", 28)
+                te = firsts(l32, [vcp(l32, told["u"], [told["t"]])])
+        send(mate, T.sa[:, a0:a0 + 448], T.sh[:, a0:a0 + 448], "ar%d" % n)
         if n == 0:
+            scp(T.tp2[:, 0:448], T.iot[:], [tIOT])
+            tTP = scp(T.tp2[:, 448:896], T.iot[:], [tIOT])
             tQE = quant(T.qe, T.se, 0, 512, T.et[:], [tE])
             tQV = quant(T.qv, T.sv, 0, 128, T.vt[:], [LV])
-            te = digits(T.tin[:], [TL])
-            thl[1] = scp(hlin[1], T.iot[:].indirect(tu), [ttu])
-        elif n == 1:
-            l32 = cols("i", 28)
-            te = digits(l32, [vcp(l32, told["u"], [told["t"]])])
         if n < 2:
-            gs = scp(lin(HS_), tinv(n).indirect(te["x"]), [tTI[n], te["tx"], lastT[HS_]])
             sibling(n + 1, [gs])
-        need("s", ("ml%d" % n, eng), ("lane", 16 * (n + 1)))
+        need("s", ("ml%d" % n, eng), ("lane", 48 * n + 16))
         am0, am1 = T.ma[:, 64 * n:64 * n + 28], T.ma[:, 64 * n + 32:64 * n + 60]
         t = scp(G[2], G[1].indirect(am1), [tg2])
         tlt = scp(lin(LT_ + n), G[2].indirect(am0), [t, pads])
@@ -354,19 +361,25 @@ def rank_program(g, core, T, topo):
             thl[2] = tlt
         if n < 2:
             tTI.append(vcp(tinv(n + 1).indirect(tn), T.iot[:], [tl]))
-        tdp = []
-        for h in range(2):
-            c0, c1 = RUNS[h]
-            need("t", ("ar%d%d" % (n, h), 2 * eng))
-            td = [mm(b + 4 * h, c1 - c0, T.qe[:, 128 * b:128 * b + 128], T.se[:, 128 * b:128 * b + 128],
-                     T.qa[:, a0 + c0:a0 + c1], T.sa[:, a0 + c0:a0 + c1], [tQE]) for b in range(4)]
-            for b in range(4):
-                r = scp(T.dp[:, x0 + 448 * b + c0:x0 + 448 * b + c1], bank(b + 4 * h, c1 - c0), [td[b]])
+            need("y", tTI[n + 1], tTP)
+            r = 448 * (n + 1)
+            Y.dma_start(T.tp2[0::16, r - 448:r], T.tinv[0::16, r:r + 448]).then_inc(T.sem.lane, 16)
+            Y.dma_start(T.tp2[1::16, r - 448:r - 1], T.tinv[1::16, r + 1:r + 448]).then_inc(T.sem.lane, 16)
+        tdp = [[], [], [], []]
+        need("t", ("ar%d" % n, 3 * eng))
+        for b in range(4):
+            for h in range(2):
+                c0, c1 = RUNS[h]
+                t = mm(b + 4 * h, c1 - c0, T.qe[:, 128 * b:128 * b + 128], T.se[:, 128 * b:128 * b + 128],
+                       T.qa[:, a0 + c0:a0 + c1], T.sa[:, a0 + c0:a0 + c1], [tQE])
+                r = scp(T.dp[:, x0 + 448 * b + c0:x0 + 448 * b + c1], bank(b + 4 * h, c1 - c0), [t])
                 free[b + 4 * h].append(r)
-                tdp.append(r)
+                tdp[b].append(r)
         if n < 2:
-            gl = scp(lin(LO_), tinv(n + 1).indirect(te["e"]), [tTI[n + 1], te["te"], lastT[LO_]])
-            gh = scp(lin(HI_), tinv(n + 1).indirect(te["o"]), [tTI[n + 1], te["to"], lastT[HI_]])
+            if n == 0:
+                gs = siblings(1, tn, [tl, tTI[1]])
+            need("s", ("lane", 48 * (n + 1)))
+            gl = scp(lin(LO_), T.tp2[:, a0:a0 + 448].indirect(te[0]), [te[1], lastT[LO_], tTI[n + 1]])
         else:
             need("s", tlt)
             ttp = done("s", S.activation(T.tpf[:], lin(LT_ + 2), AF.Identity, bias=224.0))
@@ -374,27 +387,29 @@ def rank_program(g, core, T, topo):
             Y.dma_start(T.tp[:, :], T.tpf[1::16, 0:448]).then_inc(T.sem.outs, 16)
         x1, a1 = x0 + 1792, a0 + 448
         sft, sgt = [], []
+
+        def meet(b, c0, c1):
+            return vtt(T.xs[:, x1 + 4 * c0 + b:x1 + 4 * c1:4],
+                       T.dp[:, x0 + 448 * b:x0 + 448 * b + 448].indirect(T.lu[:, u0 + c0 // 16:u0 + c1 // 16]),
+                       T.xs[:, x0 + 4 * c0 + b:x0 + 4 * c1:4], OP.add, [tl, tdp[b], tX[n]])
+        if n < 2:
+            tX[n + 1] = [meet(b, 0, 448) for b in range(4)]
         for h in range(2):
             c0, c1 = RUNS[h]
-            ls = T.lu[:, u0 + c0 // 16:u0 + c1 // 16]
-            ta = []
-            for b in range(4):
-                ta.append(vtt(T.xs[:, x1 + 4 * c0 + b:x1 + 4 * c1:4],
-                              T.dp[:, x0 + 448 * b:x0 + 448 * b + 448].indirect(ls),
-                              T.xs[:, x0 + 4 * c0 + b:x0 + 4 * c1:4], OP.add, [tl, tdp[b], tdp[4 + b], tX[n]]))
-            tX[n + 1] += ta
-            tQX[n + 1][h] = quant(T.qx, T.sx, a1 + c0, a1 + c1, T.xs[:, x1 + 4 * c0:x1 + 4 * c1], ta)
+            if n == 2:
+                tX[3] = [meet(b, c0, c1) for b in range(4)]
+            tQX[n + 1][h] = quant(T.qx, T.sx, a1 + c0, a1 + c1, T.xs[:, x1 + 4 * c0:x1 + 4 * c1], tX[n + 1])
             if n < 2:
                 score(n + 1, h)
-            else:
-                need("y", tQX[3][h])
-                Y.dma_start(T.oc[:, 4 * c0:4 * c1], T.qx[:, a1 + c0:a1 + c1].bitcast(dt.uint8)).then_inc(T.sem.outs, 16)
-                k = mm(4 * h, c1 - c0, T.qv[:, 0:128], T.sv[:, 0:128], T.qx[:, a1 + c0:a1 + c1], T.sx[:, a1 + c0:a1 + c1],
-                       [tQV, tQX[3][h]])
-                need("s", scp(T.yo[:, c0:c1], bank(4 * h, c1 - c0), [k]))
-                S.dma_start(T.y[:, c0:c1], T.yo[:, c0:c1]).then_inc(T.sem.outs, 16)
+                continue
+            need("y", tQX[3][h])
+            Y.dma_start(T.oc[:, 4 * c0:4 * c1], T.qx[:, a1 + c0:a1 + c1].bitcast(dt.uint8)).then_inc(T.sem.outs, 16)
+            k = mm(4 * h, c1 - c0, T.qv[:, 0:128], T.sv[:, 0:128], T.qx[:, a1 + c0:a1 + c1], T.sx[:, a1 + c0:a1 + c1],
+                   [tQV, tQX[3][h]])
+            need("s", scp(T.yo[:, c0:c1], bank(4 * h, c1 - c0), [k]))
+            S.dma_start(T.y[:, c0:c1], T.yo[:, c0:c1]).then_inc(T.sem.outs, 16)
         if n < 2:
-            outs(n + 1, gl, gh)
+            outs(n + 1, gl, None)
     for k in range(4):
         Y.dma_start(T.osc[4 * k:4 * k + 4, 0:448], T.sx[32 * k:32 * k + 4, 1344:1792]).then_inc(T.sem.outs, 16)
     need("y", ("outs", 16 * 9), ("loc", nloc[0]), ("lww", 32), ("lvv", 16), [("c" + q, cnt[q]) for q in cnt])

from concourse.mybir import dt, AluOpType, ActivationFunctionType

C = 448
STEP = [1, 2, 3]
R0 = 224
RUNS = [(0, R0), (R0, C)]
TINY, UP = 2.0 ** -91, 1024.0
LIN = 464
TW = 928
A_, B_, LO_, HI_, HS_, LT_ = 0, 1, 2, 3, 4, 5


def _sb(n, d):
    return ("sbuf", [128, n], d)


def _bf(n):
    return _sb(n, "bfloat16")


def _codes(n):
    return _sb(n, "float8_e4m3fn_x4")


def _plane(n):
    return _sb(n, "uint8")


SCRATCH = {
    "hin": _sb(28, "int32"), "tin": _sb(28, "int32"),
    "ut": _bf(512), "vt": _bf(512), "ones": _bf(512), "et": _bf(2048),
    "xs": _bf(4 * 1792), "xp": _bf(3 * 1792), "yf": _sb(3 * 1792, "float32"),
    "zt": _bf(3 * 1792), "ht": _bf(3 * 1792), "dp": _bf(3 * 1792),
    "qu": _codes(128), "su": _plane(128), "qv": _codes(128), "sv": _plane(128),
    "wq": _codes(512), "wp": _plane(512), "qe": _codes(512), "se": _plane(512),
    "qx": _codes(4 * 448), "sx": _plane(4 * 448), "qz": _codes(3 * 448), "sz": _plane(3 * 448),
    "qh": _codes(3 * 448), "sh": _plane(3 * 448), "qa": _codes(3 * 448), "sa": _plane(3 * 448),
    "sf": _sb(3 * 448, "float32"), "sg": _sb(3 * 448, "float32"), "slo": _sb(3 * 448, "float32"),
    "iot": _bf(448), "ln": _bf(8 * LIN + 16), "tt": _bf(6 * TW), "lg": _bf(11 * 448),
    "tinv": _bf(4 * 448), "tp2": _bf(2 * 448), "tsw": _bf(4 * 448),
    "seli": _sb(128, "int32"), "sel": _sb(8, "uint16"), "pg": _sb(8, "float32"),
    "li": _sb(512, "int32"), "lu": _sb(1024, "uint16"), "lf": _sb(2560, "float32"), "bt": _bf(192),
    "mu": _sb(192, "uint16"), "ma": _sb(192, "uint16"),
    "tpf": _sb(448, "float32"), "yo": _sb(448, "float32"),
    "ps": ("psum", [128, 4096], "float32"),
}
SEMAPHORES = (["cv", "cs", "ct", "cp", "loc", "ltl", "lhl", "lxx", "luu", "lww", "lvv", "lane", "outs"]
              + ["ml%d" % n for n in range(3)] + ["ar%d" % n for n in range(3)])


def rank_program(g, core, T, topo):
    rank = T.rank_of(core)
    if rank is None:
        return
    OP, AF = AluOpType, ActivationFunctionType
    V, S, PE, Y = g.vector, g.scalar, g.tensor, g.sync
    Q = {"v": V, "s": S, "t": PE, "p": g, "y": Y}
    cnt = {"v": 0, "s": 0, "t": 0, "p": 0}
    seen = {q: {} for q in Q}
    ncl = {"i": 0, "u": 0, "f": 0}
    tabs = {"i": T.li, "u": T.lu, "f": T.lf}

    def need(q, *toks):
        best = {}
        for t in toks:
            for a in (t if isinstance(t, list) else [t]):
                if a is not None:
                    best[a[0]] = max(best.get(a[0], 0), a[1])
        for k, v in best.items():
            if seen[q].get(k, 0) < v:
                Q[q].wait_ge(T.sem[k], v)
                seen[q][k] = v

    def done(q, inst):
        cnt[q] += 1
        inst.then_inc(T.sem["c" + q], 1)
        return ("c" + q, cnt[q])

    def take(k, n):
        a = ncl[k]
        ncl[k] = a + n
        return a

    def cols(k, n):
        a = take(k, n)
        return tabs[k][:, a:a + n]

    def vts(out, in0, s1, op0, deps, s2=None, op1=None):
        need("v", *deps)
        if op1 is None:
            return done("v", V.tensor_scalar(out, in0, s1, None, op0))
        return done("v", V.tensor_scalar(out, in0, s1, s2, op0, op1))

    def vtt(out, in0, in1, op, deps):
        need("v", *deps)
        return done("v", V.tensor_tensor(out, in0, in1, op))

    def vcp(out, in_, deps):
        need("v", *deps)
        return done("v", V.tensor_copy(out, in_))

    def scp(out, in_, deps, scale=None):
        need("s", *deps)
        if scale is None:
            return done("s", S.activation(out, in_, AF.Copy))
        return done("s", S.activation(out, in_, AF.Copy, scale=scale))

    def quant(qb, sb, a, b, tile, deps):
        need("v", *deps)
        return done("v", V.quantize_mx(qb[:, a:b], sb[:, a:b], tile))

    free = [[] for _ in range(8)]

    def mm(k, n, l, ls, r, rs, deps):
        need("t", free[k], *deps)
        free[k] = []
        return done("t", PE.matmul_mx(T.ps[:, 512 * k:512 * k + n], l, ls, r, rs, True, True))

    def bank(k, n):
        return T.ps[:, 512 * k:512 * k + n]

    def lin(k):
        return T.ln[:, LIN * k + 16:LIN * k + LIN]

    Y.dma_start(T.tin[:], T.tl[:, :]).then_inc(T.sem.ltl, 16)
    Y.dma_start(T.xs[:, 0:1792], T.x[:, :]).then_inc(T.sem.lxx, 16)
    S.dma_start(T.hin[:], T.hl[:, :]).then_inc(T.sem.lhl, 16)
    S.dma_start(T.ut[:], T.u[:, :]).then_inc(T.sem.luu, 16)
    S.dma_start(T.wq[:, 0:512].bitcast(dt.uint8), T.wc[:, :]).then_inc(T.sem.lww, 16)
    S.dma_start(T.wp[:], T.ws[:, :]).then_inc(T.sem.lww, 16)
    S.dma_start(T.vt[:], T.v[:, :]).then_inc(T.sem.lvv, 16)
    TL, HL, LX, LU, LW, LV = ("ltl", 16), ("lhl", 16), ("lxx", 16), ("luu", 16), ("lww", 32), ("lvv", 16)

    def si(k):
        return T.seli[:, 8 * k:8 * k + 8]
    iP = done("p", g.iota(si(0), [[0, 8]], 0, 1))
    iC = done("p", g.iota(si(1), [[0, 4], [16, 2]], 0, 0))
    iL = done("p", g.iota(si(2), [[1, 2], [0, 4]], 0, 0))
    tIOT = done("p", g.iota(T.iot[:], [[1, 448]], -224, 0, allow_small_or_imprecise_dtypes=True))
    iw0 = cols("f", 64)
    iW = done("p", g.iota(iw0, [[0, 2], [16, 32]], -224, 1, allow_small_or_imprecise_dtypes=True))
    tONE = done("v", V.memset(T.ones[:], 1.0))
    pads = None
    for k in range(9):
        pads = done("v", V.memset(T.ln[:, LIN * k:LIN * k + 16], 0.0))
    for b in range(4):
        need("p", tONE)
        tE = done("p", g.affine_select(T.et[:, 512 * b:512 * b + 512], T.ones[:], [[1, 512]], OP.is_equal, 0.0, -b, -4))
    a1 = vts(si(3), si(0), 15, OP.bitwise_and, [iP])
    a2 = vts(si(4), si(0), 16, OP.bitwise_and, [iP])
    a3 = vts(si(5), si(0), 4, OP.arith_shift_right, [iP])
    a4 = vtt(si(6), si(1), si(3), OP.add, [iC, a1])
    a5 = vtt(si(7), si(0), si(5), OP.add, [iP, a3])
    a6 = vtt(si(8), si(4), si(2), OP.add, [iL, a2])
    a7 = vts(si(9), si(7), 1, OP.bitwise_and, [a5])
    a8 = vtt(si(10), si(6), si(9), OP.add, [a4, a7])
    a9 = vts(si(11), si(9), 448, OP.mult, [a7])
    a10 = vts(si(12), si(10), 1, OP.arith_shift_right, [a8])
    a11 = vtt(si(13), si(8), si(11), OP.add, [a6, a9])
    a12 = vts(si(14), si(12), 32, OP.mult, [a10])
    a13 = vtt(T.pg[:], si(0), si(3), OP.subtract, [a1])
    a14 = vtt(si(15), si(14), si(13), OP.add, [a12, a11])
    IW = cols("f", 64)
    tIW = vts(IW, iw0, T.pg[:, 0:1], OP.subtract, [iW, a13], TINY, OP.mult)
    tSEL = vts(T.sel[:], si(15), TW - 1, OP.min, [a14])
    SEL, SEL2 = T.sel[:, 2:6], T.sel[:, 0:8]

    lastT = {}
    lastSel = {}

    def turn(k, slot, deps):
        a, o = LIN * k, TW * slot
        need("v", pads, lastSel.get(slot), *deps)
        done("v", V.transpose(T.tt[:, o:o + 448], T.ln[:, a + 16:a + 464]))
        t2 = done("v", V.transpose(T.tt[:, o + 448:o + TW], T.ln[:, a:a + 480]))
        lastT[k] = t2
        return t2

    def picked(slot, table=SEL):
        return T.tt[:, TW * slot:TW * slot + TW].indirect(table)

    def wrap(out, slot, deps, table=SEL):
        t = vts(out, picked(slot, table), 224.0, OP.add, [tSEL] + deps)
        lastSel[slot] = t
        return t

    def firsts(l32, deps):
        b, e, u = cols("i", 28), cols("i", 28), cols("u", 28)
        t1 = vts(b, l32, 1, OP.bitwise_and, deps)
        t2 = vtt(e, l32, b, OP.subtract, [t1])
        return u, vcp(u, e, [t2])

    tab = [{}, {}, {}]

    def sibling(n, deps):
        d = tab[n]
        t = turn(HS_, HS_, deps)
        a = take("u", 64)
        d["hs"], d["th"] = T.lu[:, a:a + 28], cols("f", 64)
        d["ths"] = vts(T.lu[:, a:a + 64], picked(HS_), 1.0 / TINY, OP.mult, [tSEL, t], 224.0, OP.add)
        d["tth"] = vtt(d["th"], picked(HS_), IW, OP.subtract, [t, tIW])
        lastSel[HS_] = d["tth"]

    def outs(n, gl, gh):
        d = tab[n]
        a = take("f", 256)
        p, q = T.lf[:, a:a + 64], T.lf[:, a + 64:a + 128]
        t1 = turn(LO_, LO_, [gl])
        if gh is None:
            t1 = t2 = wrap(T.lf[:, a:a + 128], LO_, [t1], SEL2)
        else:
            t2 = turn(HI_, HI_, [gh])
            t1 = wrap(p, LO_, [t1])
            t2 = wrap(q, HI_, [t2])
        d["LO"], d["HI"] = T.lf[:, a + 128:a + 192], T.lf[:, a + 192:a + 256]
        d["tLO"] = vtt(d["LO"], p, q, OP.min, [t1, t2])
        d["tHI"] = vtt(d["HI"], p, q, OP.max, [t1, t2])
        d["lo"], d["hi"] = cols("u", 28), cols("u", 28)
        d["tlo"] = vcp(d["lo"], T.lf[:, a + 128:a + 156], [d["tLO"]])
        d["thi"] = vcp(d["hi"], T.lf[:, a + 192:a + 220], [d["tHI"]])

    def tinv(k):
        return T.tinv[:, 448 * k:448 * k + 448]

    def siblings(k, u, deps):
        o = 448 * k
        t1 = scp(T.tsw[:, o:o + 448:2], T.tinv[:, o + 1:o + 448:2], deps)
        t2 = scp(T.tsw[:, o + 1:o + 448:2], T.tinv[:, o:o + 448:2], deps)
        return scp(lin(HS_), T.tsw[:, o:o + 448].indirect(u), [t1, t2, pads, lastT.get(HS_)], scale=TINY)

    hlin = [T.lg[:, 448 * 9:448 * 10], T.lg[:, 448 * 10:448 * 11]]
    hrow = [T.lg[1::16, 448 * 9:448 * 10], T.lg[1::16, 448 * 10:448 * 11], T.ln[1::16, LIN * LT_ + 16:LIN * LT_ + LIN]]
    tu, hu = cols("u", 28), cols("u", 28)
    ttu = vcp(tu, T.tin[:], [TL])
    thu = vcp(hu, T.hin[:], [HL])
    thl = [scp(hlin[0], T.iot[:].indirect(hu), [thu, tIOT]), scp(hlin[1], T.iot[:].indirect(tu), [ttu]), None]
    he, the = firsts(T.hin[:], [HL])
    ho = cols("u", 28)
    tho = vts(ho, he, 1.0, OP.add, [the])
    tTI = [vcp(tinv(0).indirect(tu), T.iot[:], [ttu, tIOT])]
    tHI = vcp(tinv(3).indirect(hu), T.iot[:], [thu, tIOT])
    gl = scp(lin(LO_), tinv(0).indirect(he), [tTI[0], the, pads])
    gh = scp(lin(HI_), tinv(0).indirect(ho), [tTI[0], tho])
    gs = siblings(3, hu, [tHI, thu])
    tQU = quant(T.qu, T.su, 0, 128, T.ut[:], [LU])
    tX = [[LX], [], [], []]
    tQX = [[None, None] for _ in range(4)]
    t0 = quant(T.qx, T.sx, 0, 448, T.xs[:, 0:1792], [LX])
    tQX[0] = [t0, t0]
    sft, sgt = [], []

    def score(n, h):
        c0, c1 = RUNS[h]
        a = 448 * n
        t = mm(4 * h, c1 - c0, T.qu[:, 0:128], T.su[:, 0:128], T.qx[:, a + c0:a + c1], T.sx[:, a + c0:a + c1],
               [tQU, tQX[n][h]])
        r1 = scp(T.sf[:, a + c0:a + c1], bank(4 * h, c1 - c0), [t], scale=UP)
        r2 = scp(T.sg[:, a + c0:a + c1], bank(4 * h, c1 - c0), [t], scale=UP)
        free[4 * h] += [r1, r2]
        sft.append(r1)
        sgt.append(r2)

    score(0, 0)
    score(0, 1)
    outs(0, gl, gh)
    sibling(0, [gs])

    nloc = [0]
    told = {}

    def send(dst, out, in_, sem):
        rid, pid, _ = topo.addr(dst)
        g.remote_dma(out, in_, T.sem[sem], T.sem.loc, pid, rid, topo.mask(core, dst))
        nloc[0] += len(topo.engines(core, dst))

    for n in range(3):
        d = tab[n]
        mate = T.cores[rank ^ STEP[n]]
        eng = len(topo.engines(core, mate))
        x0, a0 = 1792 * n, 448 * n
        sf, sg, slo = T.sf[:, a0:a0 + 448], T.sg[:, a0:a0 + 448], T.slo[:, a0:a0 + 448]
        ts = scp(slo, sf.indirect(d["lo"]), [sft, d["tlo"]])
        tXP = []
        for b in range(4):
            tXP.append(scp(T.xp[:, x0 + 448 * b:x0 + 448 * b + 448], T.xs[:, x0 + b:x0 + 1792:4], [tX[n]]))
        if n == 0:
            gs = siblings(0, tu, [ttu, tTI[0]])
        ta = vtt(lin(A_), sf.indirect(d["hs"]), sg, OP.subtract, [sft, sgt, d["ths"], lastT.get(A_), pads])
        tb = vtt(lin(B_), sf.indirect(d["hi"]), slo, OP.is_gt, [ts, d["thi"], lastT.get(B_)])
        ta = turn(A_, A_, [ta])
        tb = turn(B_, B_, [tb])
        ba = T.bt[:, 64 * n:64 * n + 64]
        t = vtt(ba, picked(A_), d["th"], OP.is_gt, [ta, d["tth"], tSEL])
        lastSel[A_] = t
        e, w, m = cols("f", 64), cols("f", 64), cols("f", 64)
        t = vtt(e, picked(B_), ba, OP.not_equal, [tb, t])
        lastSel[B_] = t
        t = vtt(w, e, d["HI"], OP.mult, [t, d["tHI"]])
        t = vtt(m, w, d["LO"], OP.max, [t, d["tLO"]])
        tm = vcp(T.mu[:, 64 * n:64 * n + 64], m, [t])
        m0, m1 = T.mu[:, 64 * n:64 * n + 28], T.mu[:, 64 * n + 32:64 * n + 60]
        need("p", tm)
        send(mate, T.ma[:, 64 * n:64 * n + 64], T.mu[:, 64 * n:64 * n + 64], "ml%d" % n)
        G = [T.lg[:, 448 * (3 * n + k):448 * (3 * n + k) + 448] for k in range(3)]
        tg1 = scp(G[0], T.iot[:].indirect(m1), [tm, tIOT])
        tz = []
        for b in range(4):
            p = x0 + 448 * b
            yp = T.yf[:, p:p + 448]
            ty = vtt(yp, T.xp[:, p:p + 448].indirect(m1), T.xs[:, x0 + b:x0 + 1792:4], OP.add, [tm, tXP[b], tX[n]])
            if b < 3:
                tz.append(scp(T.zt[:, x0 + b:x0 + 1792:4], yp.indirect(m0), [ty], scale=0.5))
            else:
                u = 64 * n + R0 // 16
                tza = vts(T.zt[:, x0 + b:x0 + 4 * R0:4], yp.indirect(T.mu[:, 64 * n:u]), 0.5, OP.mult, [ty])
                tzb = scp(T.zt[:, x0 + 4 * R0 + b:x0 + 1792:4], yp.indirect(T.mu[:, u:64 * n + 28]), [ty], scale=0.5)
        tq = [quant(T.qz, T.sz, a0, a0 + R0, T.zt[:, x0:x0 + 4 * R0], tz + [tza]),
              quant(T.qz, T.sz, a0 + R0, a0 + 448, T.zt[:, x0 + 4 * R0:x0 + 1792], tz + [tzb])]
        tg2 = scp(G[1], G[0].indirect(m0), [tg1])
        need("y", tg2, thl[n])
        Y.dma_start(T.lg[1::16, 448 * (3 * n + 1):448 * (3 * n + 2)], hrow[n]).then_inc(T.sem.lane, 16)
        for h in range(2):
            c0, c1 = RUNS[h]
            tr = [mm(b + 4 * h, c1 - c0, T.wq[:, 128 * b:128 * b + 128], T.wp[:, 128 * b:128 * b + 128],
                     T.qz[:, a0 + c0:a0 + c1], T.sz[:, a0 + c0:a0 + c1], [LW, tq[h]]) for b in range(4)]
            th = []
            for b in range(4):
                o = T.ht[:, x0 + 4 * c0 + b:x0 + 4 * c1:4]
                if h == 0 and b < 2:
                    r = vts(o, bank(b + 4 * h, c1 - c0), 0.03125, OP.mult, [tr[b]])
                else:
                    r = scp(o, bank(b + 4 * h, c1 - c0), [tr[b]], scale=0.03125)
                free[b + 4 * h].append(r)
                th.append(r)
            r = quant(T.qh, T.sh, a0 + c0, a0 + c1, T.ht[:, x0 + 4 * c0:x0 + 4 * c1], th)
            need("p", r)
            send(mate, T.qa[:, a0 + c0:a0 + c1].bitcast(dt.uint8), T.qh[:, a0 + c0:a0 + c1].bitcast(dt.uint8), "ar%d" % n)
            if h == 0 and n == 0:
                te = firsts(T.tin[:], [TL])
            elif h == 0 and n == 1:
                l32 = cols("i", 28)
                te = firsts(l32, [vcp(l32, told["u"], [told["t"]])])
        send(mate, T.sa[:, a0:a0 + 448], T.sh[:, a0:a0 + 448], "ar%d" % n)
        if n == 0:
            scp(T.tp2[:, 0:448], T.iot[:], [tIOT])
            tTP = scp(T.tp2[:, 448:896], T.iot[:], [tIOT])
            tQE = quant(T.qe, T.se, 0, 512, T.et[:], [tE])
            tQV = quant(T.qv, T.sv, 0, 128, T.vt[:], [LV])
        if n < 2:
            sibling(n + 1, [gs])
        need("s", ("ml%d" % n, eng), ("lane", 48 * n + 16))
        am0, am1 = T.ma[:, 64 * n:64 * n + 28], T.ma[:, 64 * n + 32:64 * n + 60]
        t = scp(G[2], G[1].indirect(am1), [tg2])
        tlt = scp(lin(LT_ + n), G[2].indirect(am0), [t, pads])
        t = turn(LT_ + n, LT_, [tlt])
        u0 = take("u", 64)
        tl = wrap(T.lu[:, u0:u0 + 64], LT_, [t])
        tn = T.lu[:, u0 + 32:u0 + 60]
        told = {"u": tn, "t": tl}
        if n == 0:
            thl[2] = tlt
        if n < 2:
            tTI.append(vcp(tinv(n + 1).indirect(tn), T.iot[:], [tl]))
            need("y", tTI[n + 1], tTP)
            r = 448 * (n + 1)
            Y.dma_start(T.tp2[0::16, r - 448:r], T.tinv[0::16, r:r + 448]).then_inc(T.sem.lane, 16)
            Y.dma_start(T.tp2[1::16, r - 448:r - 1], T.tinv[1::16, r + 1:r + 448]).then_inc(T.sem.lane, 16)
        tdp = [[], [], [], []]
        need("t", ("ar%d" % n, 3 * eng))
        for b in range(4):
            for h in range(2):
                c0, c1 = RUNS[h]
                t = mm(b + 4 * h, c1 - c0, T.qe[:, 128 * b:128 * b + 128], T.se[:, 128 * b:128 * b + 128],
                       T.qa[:, a0 + c0:a0 + c1], T.sa[:, a0 + c0:a0 + c1], [tQE])
                r = scp(T.dp[:, x0 + 448 * b + c0:x0 + 448 * b + c1], bank(b + 4 * h, c1 - c0), [t])
                free[b + 4 * h].append(r)
                tdp[b].append(r)
        if n < 2:
            if n == 0:
                gs = siblings(1, tn, [tl, tTI[1]])
            need("s", ("lane", 48 * (n + 1)))
            gl = scp(lin(LO_), T.tp2[:, a0:a0 + 448].indirect(te[0]), [te[1], lastT[LO_], tTI[n + 1]])
        else:
            need("s", tlt)
            ttp = done("s", S.activation(T.tpf[:], lin(LT_ + 2), AF.Identity, bias=224.0))
            need("y", ttp)
            Y.dma_start(T.tp[:, :], T.tpf[1::16, 0:448]).then_inc(T.sem.outs, 16)
        x1, a1 = x0 + 1792, a0 + 448
        sft, sgt = [], []

        def meet(b, c0, c1):
            return vtt(T.xs[:, x1 + 4 * c0 + b:x1 + 4 * c1:4],
                       T.dp[:, x0 + 448 * b:x0 + 448 * b + 448].indirect(T.lu[:, u0 + c0 // 16:u0 + c1 // 16]),
                       T.xs[:, x0 + 4 * c0 + b:x0 + 4 * c1:4], OP.add, [tl, tdp[b], tX[n]])
        if n < 2:
            tX[n + 1] = [meet(b, 0, 448) for b in range(4)]
        for h in range(2):
            c0, c1 = RUNS[h]
            if n == 2:
                tX[3] = [meet(b, c0, c1) for b in range(4)]
            tQX[n + 1][h] = quant(T.qx, T.sx, a1 + c0, a1 + c1, T.xs[:, x1 + 4 * c0:x1 + 4 * c1], tX[n + 1])
            if n < 2:
                score(n + 1, h)
                continue
            need("y", tQX[3][h])
            Y.dma_start(T.oc[:, 4 * c0:4 * c1], T.qx[:, a1 + c0:a1 + c1].bitcast(dt.uint8)).then_inc(T.sem.outs, 16)
            k = mm(4 * h, c1 - c0, T.qv[:, 0:128], T.sv[:, 0:128], T.qx[:, a1 + c0:a1 + c1], T.sx[:, a1 + c0:a1 + c1],
                   [tQV, tQX[3][h]])
            need("s", scp(T.yo[:, c0:c1], bank(4 * h, c1 - c0), [k]))
            S.dma_start(T.y[:, c0:c1], T.yo[:, c0:c1]).then_inc(T.sem.outs, 16)
        if n < 2:
            outs(n + 1, gl, None)
    for k in range(4):
        Y.dma_start(T.osc[4 * k:4 * k + 4, 0:448], T.sx[32 * k:32 * k + 4, 1344:1792]).then_inc(T.sem.outs, 16)
    need("y", ("outs", 16 * 9), ("loc", nloc[0]), ("lww", 32), ("lvv", 16), [("c" + q, cnt[q]) for q in cnt])
